import numpy as np
import ml_dtypes

BF16 = ml_dtypes.bfloat16


def bf(x):
    return np.asarray(x, np.float32).astype(BF16)


def f32(x):
    return np.asarray(x, np.float32)


def f64(x):
    return np.asarray(x).astype(np.float64)


def striped(idx):
    return np.tile(idx.reshape(-1, 16).T, (8, 1))


S, K, M, N, E, Q, V, D = 256, 128, 128, 192, 2, 96, 32, 8


def setup_inputs():
    return {"base": bf(np.random.standard_normal((M, S))), "x": bf(np.random.standard_normal((K, N))), "w": bf(1.5 * np.random.standard_normal((E, K, M)) / np.sqrt(K)), "b": f32(0.5 * np.random.standard_normal((M, 1))), "offs": striped(np.random.permutation(S)[:N])}


def reference(base, x, w, b, offs):
    idx = offs[:16].T.reshape(-1)
    z = f64(base).copy()
    for e in range(E):
        z[:, idx[e * Q : (e + 1) * Q]] += f64(w)[e].T @ f64(x)[:, e * Q : (e + 1) * Q]
    z = np.maximum(z + f64(b), 0.0)
    return z.reshape(M, V, D).mean(axis=2)

@@ -1,0 +1,59 @@
+import concourse.mybir as mybir
+from concourse.masks import make_identity
+
+P = 128
+CELLS = 256
+POINTS = 192
+SENSORS = 2
+PIECE = POINTS // SENSORS
+DEPTH = 8
+POOLED = CELLS // DEPTH
+
+BF16, F32, U16 = mybir.dt.bfloat16, mybir.dt.float32, mybir.dt.uint16
+ADD, MAX = mybir.AluOpType.add, mybir.AluOpType.max
+
+FLOPS = 2 * P * P * POINTS + 3 * P * CELLS
+
+
+def tile_rows_unpool_mean_relu_kernel(tc, base, x, w, b, offs, out):
+    nc = tc.nc
+    with (
+        tc.tile_pool(name="held", bufs=1) as held,
+        tc.psum_pool(name="psum", bufs=1) as psum,
+    ):
+        offsets = held.tile([P, POINTS // 16], U16, name="offsets")
+        base_sb = held.tile([P, CELLS], BF16, name="base_sb")
+        points = held.tile([P, POINTS], BF16, name="points")
+        weights = held.tile([P, SENSORS, P], BF16, name="weights")
+        bias = held.tile([P, 1], F32, name="bias")
+        ident = held.tile([P, P], BF16, name="ident")
+        cells = held.tile([P, CELLS], F32, name="cells")
+        sums = held.tile([P, POOLED], F32, name="sums")
+        means = held.tile([P, POOLED], F32, name="means")
+        window = psum.tile([P, CELLS], F32, name="window")
+
+        nc.sync.dma_start(base_sb[:], base)
+        nc.sync.dma_start(offsets[:], offs)
+        nc.sync.dma_start(points[:], x)
+        nc.sync.dma_start(weights[:], w.rearrange("e k m -> k e m"))
+        nc.scalar.dma_start(bias[:], b)
+        make_identity(nc, ident[:])
+
+        nc.tensor.matmul(window[:], ident[:], base_sb[:], start=True, stop=False)
+        for sensor in range(SENSORS):
+            piece = slice(sensor * PIECE, (sensor + 1) * PIECE)
+            places = offsets[:, sensor * PIECE // 16 : (sensor + 1) * PIECE // 16]
+            nc.tensor.matmul(
+                window[:].indirect(places),
+                weights[:, sensor, :],
+                points[:, piece],
+                start=False,
+                stop=sensor == SENSORS - 1,
+            )
+
+        nc.vector.tensor_scalar(cells[:], window[:], bias[:], 0.0, op0=ADD, op1=MAX)
+        nc.vector.tensor_reduce(
+            sums[:], cells[:].rearrange("p (v d) -> p v d", d=DEPTH), mybir.AxisListType.X, ADD
+        )
+        nc.vector.tensor_scalar_mul(means[:], sums[:], 1.0 / DEPTH)
+        nc.sync.dma_start(out, means[:])

@@ -10,7 +10,8 @@ DEPTH = 8
 POOLED = CELLS // DEPTH
 
 BF16, F32, U16 = mybir.dt.bfloat16, mybir.dt.float32, mybir.dt.uint16
-ADD, MAX = mybir.AluOpType.add, mybir.AluOpType.max
+ADD = mybir.AluOpType.add
+RELU = mybir.ActivationFunctionType.Relu
 
 FLOPS = 2 * P * P * POINTS + 3 * P * CELLS
 
@@ -26,9 +27,10 @@ def tile_rows_unpool_mean_relu_kernel(tc, base, x, w, b, offs, out):
         points = held.tile([P, POINTS], BF16, name="points")
         weights = held.tile([P, SENSORS, P], BF16, name="weights")
         bias = held.tile([P, 1], F32, name="bias")
+        bias_share = held.tile([P, 1], F32, name="bias_share")
+        first = held.tile([P, 1], F32, name="first")
         ident = held.tile([P, P], BF16, name="ident")
         cells = held.tile([P, CELLS], F32, name="cells")
-        sums = held.tile([P, POOLED], F32, name="sums")
         means = held.tile([P, POOLED], F32, name="means")
         window = psum.tile([P, CELLS], F32, name="window")
 
@@ -38,6 +40,11 @@ def tile_rows_unpool_mean_relu_kernel(tc, base, x, w, b, offs, out):
         nc.sync.dma_start(weights[:], w.rearrange("e k m -> k e m"))
         nc.scalar.dma_start(bias[:], b)
         make_identity(nc, ident[:])
+
+        nc.vector.memset(first[:], 0.0)
+        nc.scalar.activation(first[:], first[:], RELU)
+
+        nc.vector.tensor_scalar_mul(bias_share[:], bias[:], 1.0 / DEPTH)
 
         nc.tensor.matmul(window[:], ident[:], base_sb[:], start=True, stop=False)
         for sensor in range(SENSORS):
@@ -51,9 +58,8 @@ def tile_rows_unpool_mean_relu_kernel(tc, base, x, w, b, offs, out):
                 stop=sensor == SENSORS - 1,
             )
 
-        nc.vector.tensor_scalar(cells[:], window[:], bias[:], 0.0, op0=ADD, op1=MAX)
+        nc.scalar.activation(cells[:], window[:], RELU, bias=bias_share[:], scale=1.0 / DEPTH)
         nc.vector.tensor_reduce(
-            sums[:], cells[:].rearrange("p (v d) -> p v d", d=DEPTH), mybir.AxisListType.X, ADD
+            means[:], cells[:].rearrange("p (v d) -> p v d", d=DEPTH), mybir.AxisListType.X, ADD
         )
-        nc.vector.tensor_scalar_mul(means[:], sums[:], 1.0 / DEPTH)
         nc.sync.dma_start(out, means[:])

@@ -8,6 +8,7 @@ SENSORS = 2
 PIECE = POINTS // SENSORS
 DEPTH = 8
 POOLED = CELLS // DEPTH
+WARM_UPS = 7
 
 BF16, F32, U16 = mybir.dt.bfloat16, mybir.dt.float32, mybir.dt.uint16
 ADD = mybir.AluOpType.add
@@ -33,6 +34,8 @@ def tile_rows_unpool_mean_relu_kernel(tc, base, x, w, b, offs, out):
         cells = held.tile([P, CELLS], F32, name="cells")
         means = held.tile([P, POOLED], F32, name="means")
         window = psum.tile([P, CELLS], F32, name="window")
+        zeros = held.tile([P, CELLS], BF16, name="zeros")
+        spare = psum.tile([P, CELLS], F32, name="spare")
 
         nc.sync.dma_start(base_sb[:], base)
         nc.sync.dma_start(offsets[:], offs)
@@ -40,11 +43,14 @@ def tile_rows_unpool_mean_relu_kernel(tc, base, x, w, b, offs, out):
         nc.sync.dma_start(weights[:], w.rearrange("e k m -> k e m"))
         nc.scalar.dma_start(bias[:], b)
         make_identity(nc, ident[:])
+        nc.vector.memset(zeros[:], 0.0)
 
-        nc.vector.memset(first[:], 0.0)
-        nc.scalar.activation(first[:], first[:], RELU)
+        nc.scalar.activation(first[:], zeros[:, 0:1], RELU)
 
         nc.vector.tensor_scalar_mul(bias_share[:], bias[:], 1.0 / DEPTH)
+
+        for warm_up in range(WARM_UPS):
+            nc.tensor.matmul(spare[:], zeros[:, 0:P], zeros[:], start=True, stop=True)
 
         nc.tensor.matmul(window[:], ident[:], base_sb[:], start=True, stop=False)
         for sensor in range(SENSORS):

@@ -40,7 +40,7 @@ def tile_rows_unpool_mean_relu_kernel(tc, base, x, w, b, offs, out):
         nc.sync.dma_start(base_sb[:], base)
         nc.sync.dma_start(offsets[:], offs)
         nc.sync.dma_start(points[:], x)
-        nc.sync.dma_start(weights[:], w.rearrange("e k m -> k e m"))
+        nc.scalar.dma_start(weights[:], w.rearrange("e k m -> k e m"))
         nc.scalar.dma_start(bias[:], b)
         make_identity(nc, ident[:])
         nc.vector.memset(zeros[:], 0.0)

@@ -64,8 +64,11 @@ def tile_rows_unpool_mean_relu_kernel(tc, base, x, w, b, offs, out):
                 stop=sensor == SENSORS - 1,
             )
 
-        nc.scalar.activation(cells[:], window[:], RELU, bias=bias_share[:], scale=1.0 / DEPTH)
-        nc.vector.tensor_reduce(
-            means[:], cells[:].rearrange("p (v d) -> p v d", d=DEPTH), mybir.AxisListType.X, ADD
-        )
+        for half in range(2):
+            wide = slice(half * CELLS // 2, (half + 1) * CELLS // 2)
+            narrow = slice(half * POOLED // 2, (half + 1) * POOLED // 2)
+            nc.scalar.activation(cells[:, wide], window[:, wide], RELU, bias=bias_share[:], scale=1.0 / DEPTH)
+            nc.vector.tensor_reduce(
+                means[:, narrow], cells[:, wide].rearrange("p (v d) -> p v d", d=DEPTH), mybir.AxisListType.X, ADD
+            )
         nc.sync.dma_start(out, means[:])

import concourse.mybir as mybir
from concourse.masks import make_identity

P = 128
CELLS = 256
POINTS = 192
SENSORS = 2
PIECE = POINTS // SENSORS
DEPTH = 8
POOLED = CELLS // DEPTH
WARM_UPS = 7

BF16, F32, U16 = mybir.dt.bfloat16, mybir.dt.float32, mybir.dt.uint16
ADD = mybir.AluOpType.add
RELU = mybir.ActivationFunctionType.Relu

FLOPS = 2 * P * P * POINTS + 3 * P * CELLS


def tile_rows_unpool_mean_relu_kernel(tc, base, x, w, b, offs, out):
    nc = tc.nc
    with (
        tc.tile_pool(name="held", bufs=1) as held,
        tc.psum_pool(name="psum", bufs=1) as psum,
    ):
        offsets = held.tile([P, POINTS // 16], U16, name="offsets")
        base_sb = held.tile([P, CELLS], BF16, name="base_sb")
        points = held.tile([P, POINTS], BF16, name="points")
        weights = held.tile([P, SENSORS, P], BF16, name="weights")
        bias = held.tile([P, 1], F32, name="bias")
        bias_share = held.tile([P, 1], F32, name="bias_share")
        first = held.tile([P, 1], F32, name="first")
        ident = held.tile([P, P], BF16, name="ident")
        cells = held.tile([P, CELLS], F32, name="cells")
        means = held.tile([P, POOLED], F32, name="means")
        window = psum.tile([P, CELLS], F32, name="window")
        zeros = held.tile([P, CELLS], BF16, name="zeros")
        spare = psum.tile([P, CELLS], F32, name="spare")

        nc.sync.dma_start(base_sb[:], base)
        nc.sync.dma_start(offsets[:], offs)
        nc.sync.dma_start(points[:], x)
        nc.scalar.dma_start(weights[:], w.rearrange("e k m -> k e m"))
        nc.scalar.dma_start(bias[:], b)
        make_identity(nc, ident[:])
        nc.vector.memset(zeros[:], 0.0)

        nc.scalar.activation(first[:], zeros[:, 0:1], RELU)

        nc.vector.tensor_scalar_mul(bias_share[:], bias[:], 1.0 / DEPTH)

        for warm_up in range(WARM_UPS):
            nc.tensor.matmul(spare[:], zeros[:, 0:P], zeros[:], start=True, stop=True)

        nc.tensor.matmul(window[:], ident[:], base_sb[:], start=True, stop=False)
        for sensor in range(SENSORS):
            piece = slice(sensor * PIECE, (sensor + 1) * PIECE)
            places = offsets[:, sensor * PIECE // 16 : (sensor + 1) * PIECE // 16]
            nc.tensor.matmul(
                window[:].indirect(places),
                weights[:, sensor, :],
                points[:, piece],
                start=False,
                stop=sensor == SENSORS - 1,
            )

        for half in range(2):
            wide = slice(half * CELLS // 2, (half + 1) * CELLS // 2)
            narrow = slice(half * POOLED // 2, (half + 1) * POOLED // 2)
            nc.scalar.activation(cells[:, wide], window[:, wide], RELU, bias=bias_share[:], scale=1.0 / DEPTH)
            nc.vector.tensor_reduce(
                means[:, narrow], cells[:, wide].rearrange("p (v d) -> p v d", d=DEPTH), mybir.AxisListType.X, ADD
            )
        nc.sync.dma_start(out, means[:])
